import numpy as np, ml_dtypes
CORES = [16,17,18,19,32,33,34,35]
N = 8
BF = ml_dtypes.bfloat16
P, G, RO, C, J = 2048, 256, 2, 3, 3
W = P + (N - 1) * G
def parts(rng):
    w = rng.choice(np.array([4, 12, 40]), (N, 8, 1, 1))
    r = (120 * rng.random((N, 8, 1, P)) + w * rng.random((N, 8, 16, P))).astype(np.int64)
    v = (60 + 150 * rng.random((N, 8, 1, P)) + w * rng.random((N, 8, 16, P))).astype(np.int64)
    m = np.minimum(rng.poisson(0.4 + 0.35 * rng.random((N, 8, 1, 1, 16)), (N, 8, 16, 16, 16)), 15)
    low = rng.random((N, 8, 16, P)) < rng.choice(np.array([0.2, 0.5, 0.8]), (N, 8, 1, 1))
    s = np.where(low, rng.integers(0, G, low.shape), rng.integers(0, W, low.shape))
    return v, r, m, s
def pack(v, r, m, s):
    return {"v0": np.ascontiguousarray(v.reshape(N, 128, P)).astype(np.float32).astype(BF), "rew": np.ascontiguousarray(r.reshape(N, 128, P)).astype(np.float32).astype(BF),
            "mat": np.ascontiguousarray(m.reshape(N, 128, 256)).astype(np.float32).astype(BF), "succ": np.ascontiguousarray(s.reshape(N, 128, P)).astype(np.int32)}
def setup_inputs(rng):
    return pack(*parts(rng))
def near(rng, base):
    u = rng.integers(0, 4, (N, 8, 1, P)); i1 = rng.integers(0, 16, u.shape); i2 = (i1 + rng.integers(1, 16, u.shape)) % 16; st = np.arange(16)[:, None]
    return base + ((st == i1) & (u % 2 == 1)) - ((st == i2) & (u >= 2))
def setup_inputs_ties(rng):
    v, r, m, s = parts(rng); base = rng.integers(50, 201, (1, 8, 16, 1))
    r = near(rng, base); v = near(rng, base); m[:, :4] = 0; m[:, 4:6, :, 1::2] = 0; r[:, 4:] = r[:, 4:] >> 1
    return pack(v, r, m, s)
def setup_inputs_chains(rng):
    v, r, m, s = parts(rng); m[:, ::2] = 0
    o = np.argsort(rng.random((N, 8, P)), axis=-1); at = np.argsort(o, axis=-1)
    r = (at[:, :, None, :] + np.arange(16)[:, None]) >> 4; v = np.array(r)
    up = np.where(at == P - 1, rng.integers(P, W, at.shape), np.take_along_axis(o, np.minimum(at + 1, P - 1), 2)); down = np.take_along_axis(o, np.maximum(at - 1, 0), 2)
    v[0, ::4, :, :G] = P // 16 + 6
    for a in range(1, N): up[a, ::4] = np.where(at[a, ::4] == P - 1, P + (N - 1 - a) * G + up[a, ::4] % G, up[a, ::4])
    s[:, :, ::2] = up[:, :, None, :]
    s[:, 2::4, 0] = down[:, 2::4]; s[:, 3::4, 0] = down[:, 3::4]
    s[:, 2::4, 1::2] = rng.integers(G, W, s[:, 2::4, 1::2].shape)
    return pack(v, r, m, s)
def setup_inputs_alike(rng):
    v, r, m, s = parts(rng)
    s[:, 0] = rng.choice(np.array([0, P - 1, P, W - 1, G - 1, G]), (N, 16, P))
    s[:, 1] = np.arange(P)
    s[:, 2] = rng.integers(P, W, (N, 16, P))
    s[:, 3] = rng.integers(0, G, (N, 16, P))
    s[:, 4] = s[:, 4, :1]
    v[:, 5] = rng.integers(1, 200, (N, 1, 1))
    s[:, 6] = rng.integers(0, 8, (N, 16, P))
    return pack(v, r, m, s)
def setup_inputs_full(rng):
    v, r, m, s = parts(rng)
    r[:, 0] = 255
    r[:, 1] = 0; v[:, 1] = 0
    m[:, 2] = 15; v[:, 2] = rng.integers(0, 3, (N, 16, P))
    v[:, 3] = 0; v[rng.integers(0, N), 3] = 255
    v[:, 4] = 255 * rng.integers(0, 2, (N, 16, P)); r[:, 4] = rng.choice(np.array([0, 254, 255]), (N, 16, P))
    m[:, 5] = 0; m[:, 5, 0, :2] = 1; v[:, 5, 0] = rng.integers(126, 131, (N, P)); r[:, 5] = rng.integers(0, 2, (N, 16, P)); r[:, 5, 0] = rng.integers(126, 131, (N, P))
    m[:, 6] = 0; m[:, 6, :, 2] = rng.integers(13, 16, (N, 16, 16)); v[:, 6] = rng.integers(60, 241, (N, 1, P)) + rng.integers(0, 16, (N, 16, P)); r[:, 6] = rng.integers(0, 16, (N, 16, P))
    k = np.arange(16) != rng.integers(0, 16); h = rng.integers(0, 256, (N, 1, P))
    m[:, 7] = 0; m[:, 7, :, 1] = 15 * (k[:, None] == k[None, :]); v[:, 7] = np.where(k[:, None], h, 255 - h); r[:, 7] = rng.integers(0, 16, (N, 16, P))
    return pack(v, r, m, s)
def setup_inputs_spread(rng):
    v, r, m, s = parts(rng)
    v = np.minimum((np.exp2(8 * rng.random((N, 8, 1, P))) * rng.random((N, 8, 16, P))).astype(np.int64), 255)
    r = np.minimum((np.exp2(8 * rng.random((N, 8, 1, P))) * rng.random((N, 8, 16, P))).astype(np.int64), 255)
    m = np.minimum((16 * rng.random((N, 8, 16, 16, 16)) ** rng.choice(np.array([8, 16, 64]), (N, 8, 1, 1, 16))).astype(np.int64), 15)
    s = np.minimum((W * rng.random((N, 8, 16, P)) ** rng.choice(np.array([0.5, 1, 3]), (N, 8, 16, 1))).astype(np.int64), W - 1)
    return pack(v, r, m, s)
def check_inputs(d):
    bad = []
    for k, hi in (("v0", 255), ("rew", 255), ("mat", 15), ("succ", W - 1)):
        x = np.asarray(d[k]).astype(np.float64)
        if not (np.all(x >= 0) and np.all(x <= hi) and np.all(x == np.floor(x))): bad.append("whole numbers and range of " + k)
    return bad
def value(w, s, m, r):
    z = np.stack([m[g] @ np.take(w[g], s[g], axis=1).reshape(256, P) for g in range(8)])
    return np.minimum(255, r + np.floor(z * 2.0 ** -8))
def reference(v0, rew, mat, succ):
    v = v0.astype(np.float64).reshape(N, 8, 16, P); r = rew.astype(np.float64).reshape(N, 8, 16, P); s = succ.astype(np.int64).reshape(N, 8, 16, P)
    m = np.ascontiguousarray(mat.astype(np.float64).reshape(N, 8, 16, 16, 16).transpose(0, 1, 4, 2, 3)).reshape(N, 8, 16, 256)
    n = np.arange(P)
    for t in range(RO):
        nv, ns = [], []
        odd = ((np.arange(16) + t) & 1)[:, None] == 1
        for a in range(N):
            w = np.concatenate([v[a]] + [v[(a + d) % N][:, :, :G] for d in range(1, N)], axis=2)
            x = value(w, s[a], m[a], r[a])
            guest = (n + np.add.reduce(v[a], axis=1).astype(np.int64)) & (G - 1)
            e = np.take_along_axis(s[(a + t + 1) % N], guest[:, None, :], 2)
            c = np.where(odd, np.where(e < G, P + G * t + e, n), s[a])
            y = value(w, c, m[a], r[a])
            ok = np.all(y >= x, axis=1)[:, None, :]
            x = np.where(ok, y, x); c = np.where(ok, c, s[a])
            u = np.concatenate([x, w[:, :, P:]], axis=2); total = np.add.reduce(u, axis=1)
            D = np.tile(np.arange(W), (8, 1))
            for k in range(C - 1, -1, -1):
                h = c[:, 3 * k + t]
                good = np.all(np.take_along_axis(u, h[:, None, :], 2) >= x, axis=1) & (np.take_along_axis(total, h, 1) > total[:, :P])
                D[:, :P] = np.where(good, h, D[:, :P])
            for _ in range(J): D = np.take_along_axis(D, D, 1)
            nv.append(x); ns.append(np.take_along_axis(D, c.reshape(8, 16 * P), 1).reshape(8, 16, P))
        v = np.stack(nv); s = np.stack(ns)
    return {"yv": v.reshape(N, 128, P).astype(np.float32).astype(BF), "ys": s.reshape(N, 128, P).astype(np.float32)}

from concourse.bass import DstId, RemoteDMATransfer
from concourse.mybir import AluOpType, ActivationFunctionType

A = AluOpType
AF = ActivationFunctionType
N, P, GH, W = 8, 2048, 256, 3840
KEY = 8192.0
HALF = 255.0 / 512.0
PRM = {
    "CH": [256, 256, 256, 128, 64, 64],
    "SC": [[176, 0, 0, 0, 0, 16], [0, 0, 0, 0, 0, 16]],
    "SB": [[0, 180, 180, 100, 56, 64], [150, 160, 160, 100, 56, 64]],
    "DOM": "hs00 hv01 p0 d0 hs10 hv11 p1 d1 gs2 L p2 d2 rv00 rs01 gs3 z0 K rv10 rv11 p3 d3 z1 gv4 rs20 rs21 gs5 "
           "p4 d4 z2 rv30 rv31 p5 d5 z3 rv40 rs41 P z4 rs50 rs51 z5",
    "CV": 28,
    "SEL": 256,
    "FIN": [128] * 14 + [64] * 4,
}
NDS = 70

bf, f32, i32, u16, f16 = "bfloat16", "float32", "int32", "uint16", "float16"
SB = {
    "W0": (W, bf), "U": (W, bf), "T1": (W + P, bf), "DA": (W, bf), "DB": (W, bf), "F": (W + P, bf),
    "Rq": (P, bf), "Se": (1024, i32), "So": (1024, i32),
    "Le": (1024, u16), "Lo": (1024, u16), "Ln0": (1024, u16), "Ln1": (1024, u16), "Lc": (1024, u16),
    "cK": (1024, f32), "nK0": (1024, f32), "nK1": (1024, f32), "ramp": (256, f32), "selI": (1024, i32),
    "G0": (4096, bf), "G1": (4096, bf), "G2": (4096, bf), "G3": (4096, bf), "G4": (4096, bf), "G5": (4096, bf),
    "G6": (2048, bf), "G7": (2048, bf), "X": (P, bf),
    "aI": (1024, i32), "b16": (1024, f16), "lt": (P, bf), "cl": (3072, bf),
    "raw": (256, i32), "tu": (256, f32), "TS0": (256, bf), "TS1": (256, bf), "TG0": (256, bf), "TG1": (256, bf),
    "LgI": (128, i32), "Lg": (128, u16), "gam": (128, u16), "LP0": (512, u16), "LP1": (512, u16), "LU": (384, u16),
    "NL": (1024, u16), "ZL": (128, u16), "KP": (640, f32), "sf": (512, f32), "si": (384, i32), "HL": (256, bf),
    "ci": (4, i32), "cf": (24, f32), "val": (144, f32), "val2": (128, f32), "qg": (128, f32), "gm": (8, f32),
    "Wd": (144, bf), "WdS": (144, bf), "WdN": (144, bf), "Wd2": (144, bf), "Ip": (128, bf), "In": (128, bf),
    "I1": (128, bf), "I16": (128, f16), "BO": (128, bf), "BH": (256, bf), "CP": (256, bf), "one": (512, bf),
    "neg": (128, bf), "cz": (128, bf), "nu": (128, f32), "nl": (128, f32), "idf": (128, f32), "idb": (256, bf),
    "Y": (P, f32),
}
SCRATCH = {k: ("sbuf", [128, n], d) for k, (n, d) in SB.items()}
SCRATCH["mt"] = ("sbuf", [128, 16, 16], bf)
SCRATCH["Mb"] = ("sbuf", [128, 16, 128], bf)
SCRATCH["ps"] = ("psum", [128, 4096], f32)
SEMAPHORES = (["cv", "cs", "cp", "cg"] + ["far0", "near0", "tab0", "far1", "near1", "tab1"]
              + ["ls%d" % i for i in range(6)] + ["d%d" % i for i in range(NDS)])


def rank_program(g, core, T, topo):
    rank = T.rank_of(core)
    if rank is None:
        return
    cores = list(T.cores)
    CH = PRM["CH"]
    Q = {"v": g.vector, "s": g.scalar, "p": g.tensor, "g": g, "y": g.sync}
    own = {"v": ["cv", 0], "s": ["cs", 0], "p": ["cp", 0], "g": ["cg", 0]}
    waited = {q: {} for q in Q}
    recs = {}
    total = {}
    nds = [0]

    def v(name, lo, hi, step=1, part=None):
        t = T[name]
        ap = t[:, lo:hi:step] if step != 1 else (t[:, lo:hi] if part is None else t[part, lo:hi])
        return (ap, name, lo, hi)

    def wait(q, tok):
        if waited[q].get(tok[0], 0) < tok[1]:
            Q[q].wait_ge(T.sem[tok[0]], int(tok[1]))
            waited[q][tok[0]] = tok[1]

    def order(q, reads, writes, tok):
        new = []
        for rs, isw in ((reads, False), (writes, True)):
            for r in rs:
                if r is None or isinstance(r, (int, float)):
                    continue
                name, lo, hi = r[1], r[2], r[3]
                for (l, h, tk, w, qq) in recs.get(name, []):
                    if tk is tok:
                        continue
                    if name == "ps" and qq != q:
                        if l // 512 <= (hi - 1) // 512 and lo // 512 <= (h - 1) // 512:
                            wait(q, tk)
                    elif l < hi and lo < h and (w or isw) and not (q == "p" and qq == "p"):
                        wait(q, tk)
                new.append((name, lo, hi, isw))
        for name, lo, hi, isw in new:
            old = recs.get(name, [])
            if isw:
                old = [x for x in old if x[2] is tok or not (lo <= x[0] and x[1] <= hi)]
            else:
                old = [x for x in old if x[3] or x[4] != q or q in ("y", "g", "r") or not (lo <= x[0] and x[1] <= hi)]
            recs[name] = old + [(lo, hi, tok, isw, q)]

    def ap(x):
        return x[0] if isinstance(x, tuple) else x

    def done(q, ins):
        own[q][1] += 1
        total[own[q][0]] = own[q][1]
        ins.then_inc(T.sem[own[q][0]], 1)

    def nxt(q):
        return [own[q][0], own[q][1] + 1]

    def ts(out, in0, s1, s2, op0, op1=None):
        order("v", [in0, s1, s2], [out], nxt("v"))
        if op1 is None:
            done("v", g.vector.tensor_scalar(out[0], in0[0], ap(s1), None, op0))
        else:
            done("v", g.vector.tensor_scalar(out[0], in0[0], ap(s1), ap(s2), op0, op1))

    def tt(out, in0, in1, op):
        order("v", [in0, in1], [out], nxt("v"))
        done("v", g.vector.tensor_tensor(out[0], in0[0], in1[0], op))

    def cp(out, in_, q="v"):
        order(q, [in_], [out], nxt(q))
        if q == "v":
            done(q, g.vector.tensor_copy(out[0], in_[0]))
        else:
            done(q, g.scalar.activation(out[0], in_[0], AF.Copy))

    def act(out, in_, func, bias=None, scale=None):
        order("s", [in_, bias, scale], [out], nxt("s"))
        if scale is None:
            done("s", g.scalar.activation(out[0], in_[0], func, bias=ap(bias)))
        else:
            done("s", g.scalar.activation(out[0], in_[0], func, scale=ap(scale)))

    def iota(out, pattern, base, cm, small=True):
        order("g", [], [out], nxt("g"))
        if small:
            done("g", g.iota(out[0], pattern, base, cm, allow_small_or_imprecise_dtypes=True))
        else:
            done("g", g.iota(out[0], pattern, base, cm))

    def gather(q, out, win, off):
        if out[3] <= out[2]:
            return
        order(q, [win, off], [out], nxt(q))
        src = win[0].indirect(off[0])
        if q == "v":
            done(q, g.vector.tensor_copy(out[0], src))
        else:
            done(q, g.scalar.activation(out[0], src, AF.Copy))

    def mm(items):
        tok = nxt("p")
        for i, (out, l, r, st, sp) in enumerate(items):
            order("p", [l, r], [out], tok)
            ins = g.tensor.matmul(out[0], l[0], r[0], st, sp)
            if i == len(items) - 1:
                done("p", ins)

    def dmas(items, q="y", tok=None):
        if tok is None:
            tok = ["d%d" % nds[0], 0]
            nds[0] += 1
        for out, in_ in items:
            order(q, [in_ if isinstance(in_, tuple) else None], [out if isinstance(out, tuple) else None], tok)
        for out, in_ in items:
            Q[q].dma_start(ap(out), ap(in_)).then_inc(T.sem[tok[0]], 16)
            tok[1] += 16
        total[tok[0]] = tok[1]
        return tok

    def lands(reg, tok):
        total[tok[0]] = tok[1]
        recs[reg[1]] = recs.get(reg[1], []) + [(reg[2], reg[3], tok, True, "r")]

    nls = [0]

    def send(src, transfers):
        tok = ["ls%d" % nls[0], sum(len(e) for e, _, _ in transfers)]
        nls[0] += 1
        order("g", [src], [], tok)
        total[tok[0]] = tok[1]
        tr = []
        for eng, sem, dsts in transfers:
            ids = []
            for r, _ in dsts:
                rid, pid, _se = topo.addr(cores[r])
                ids.append(DstId(rid=rid, pnc=pid))
            tr.append(RemoteDMATransfer(dst_ids=ids, dma_engine_mask=sum(1 << e for e in eng), remote_sem=T.sem[sem],
                                        srcs=[src[0]], dsts=[d[0] for _, d in dsts]))
        g.remote_dma_fused(tr, local_sem=T.sem[tok[0]])

    def chip_ranks(r):
        return [x for x in range(N) if topo.chip(cores[x]) == topo.chip(cores[r])]

    def partner(r):
        here = chip_ranks(r)
        there = [x for x in range(N) if x not in here]
        return there[here.index(r)]

    near = [x for x in chip_ranks(rank) if x != rank]
    far = partner(rank)
    e_far = topo.engines(core, cores[far])
    e_all = topo.engines(core, cores[near[0]])
    e_near = [e for e in e_all if e not in e_far]

    def slot(name, src_rank, at_rank):
        d = (src_rank - at_rank) % N
        return v(name, P + (d - 1) * GH, P + d * GH)

    def expect(t, name):
        lands(slot(name, far, rank), ["far%d" % t, len(e_far)])
        tok = ["near%d" % t, len(near) * (len(e_near) + len(e_all))]
        for x in near:
            lands(slot(name, x, rank), tok)
            lands(slot(name, partner(x), rank), tok)
        giver = (rank + t + 1) % N
        lands(v("TG%d" % t, 0, 256), ["tab%d" % t, len(topo.engines(cores[giver], core))])
        return tok

    def ghosts_out(t, name, src):
        send(src, [(e_far, "far%d" % t, [(far, slot(name, rank, far))]),
                   (e_near, "near%d" % t, [(x, slot(name, rank, x)) for x in near])])

    def ghosts_on(t, name):
        send(slot(name, far, rank), [(e_all, "near%d" % t, [(x, slot(name, far, x)) for x in near])])

    def table_out(t):
        to = (rank - t - 1) % N
        send(v("TS%d" % t, 0, 256), [(topo.engines(core, cores[to]), "tab%d" % t, [(to, v("TG%d" % t, 0, 256))])])

    ghosts0 = expect(0, "W0")
    expect(1, "T1")

    def col(i):
        return v("cf", i, i + 1)

    def psv(b, lo, hi):
        return v("ps", 512 * b + lo, 512 * b + hi)

    def to_a(a, name="Wd"):
        return v(name, 16 - a, 144 - a)

    starts = [sum(CH[:i]) for i in range(len(CH))]
    w0 = CH[0]

    def arcs_in(name, par, lo, hi):
        return [(v(name, lo, hi, part=slice(h, 128, 2)), T.succ[par:128:2, 1024 * h + lo:1024 * h + hi]) for h in range(2)]

    def rewards_in(qs):
        return [(v("Rq", 2 * starts[q] + h * CH[q], 2 * starts[q] + (h + 1) * CH[q]),
                 T.rew[:, 1024 * h + starts[q]:1024 * h + starts[q] + CH[q]]) for q in qs for h in range(2)]

    dmas([(v("W0", 0, GH), T.v0[:, 0:GH])])
    dmas([(v("raw", 0, 256, part=slice(h, 128, 2)), T.succ[1:128:2, 0:256]) for h in range(2)])
    dmas([((T.mt[:], "mt", 0, 256), T.mat[:, :])], "s")
    dmas([(v("W0", GH, P), T.v0[:, GH:P])])
    dmas(arcs_in("Se", 0, 0, w0), "s")
    dmas(arcs_in("So", 1, 0, w0), "s")
    wait("y", ghosts0)
    dmas(arcs_in("Se", 0, w0, 1024))
    dmas(rewards_in([0]))
    dmas(arcs_in("So", 1, w0, 1024))
    dmas(rewards_in(range(1, len(CH))))
    dmas([(v("LgI", 0, 128), T.succ[0:128:2, 0:256])])

    iota(v("ci", 0, 1), [[1, 1]], 0, 1, False)
    iota(v("val", 0, 144), [[1, 144]], 0, -1)
    iota(v("qg", 0, 128), [[1, 8], [0, 16]], 0, 0)
    iota(v("ramp", 0, 256), [[1, 256]], 0, 0)
    ghosts_out(0, "W0", v("W0", 0, GH))
    ts(v("ci", 1, 2), v("ci", 0, 1), 15, None, A.bitwise_and)
    ts(v("ci", 2, 3), v("ci", 0, 1), 1, None, A.bitwise_and)
    ts(v("ci", 3, 4), v("ci", 0, 1), 4, None, A.arith_shift_right)
    cp(v("cf", 0, 4), v("ci", 0, 4))
    PM, PAR, GI = col(1), col(2), col(3)
    lines = [(PAR, -1, 256), (PAR, -255, 255), (PAR, 41, -40), (PAR, -10240, 10240),
             (PAR, -22, 23), (PAR, 5824, -5824), (PAR, -1, 0), (PAR, -1, 1), (PAR, -255, 256),
             (GI, 2, 0), (GI, 2, 1), (PAR, 1024, KEY), (PM, 112, P), (PM, 64, 0)]

    def cols(idx):
        for i in idx:
            src, m, a = lines[i]
            ts(col(4 + i), src, float(m), float(a), A.mult, A.add)

    def make_table(t, src):
        ts(v("tu", 0, 256), src, col(4), col(5), A.min, A.max)
        ts(v("TS%d" % t, 0, 256), v("tu", 0, 256), col(6 + 2 * t), col(7 + 2 * t), A.mult, A.add)
        table_out(t)

    ts(v("gm", 0, 8), v("qg", 0, 128, 16), GI, 1.0 / 256, A.is_equal, A.mult)
    cols(range(4))
    ts(v("Wd", 0, 144), v("val", 0, 144), PM, 16.0, A.add, A.is_equal)
    ts(v("nl", 0, 128), v("ramp", 0, 128), 16.0, PM, A.mult, A.add)
    make_table(0, v("raw", 0, 256))
    iota(v("val2", 0, 128), [[2, 8], [0, 8], [1, 2]], 0, 0)
    ghosts_on(0, "W0")
    for gg in range(8):
        act((T.Mb[:, :, 16 * gg:16 * gg + 16], "Mb", 0, 2048), (T.mt[:], "mt", 0, 256), AF.Identity, scale=v("gm", gg, gg + 1))

    def guests(name):
        mm([(psv(7, 0, 128), to_a(a), v(name, a, P, 16), a == 0, a == 15) for a in range(16)])
        tt(v("si", 0, 128), psv(7, 0, 128), v("nl", 0, 128), A.add)
        ts(v("si", 0, 128), v("si", 0, 128), 255, None, A.bitwise_and)
        cp(v("gam", 0, 128), v("si", 0, 128))

    act(v("WdS", 0, 144), v("Wd", 0, 144), AF.Identity, scale=2 * KEY)
    act(v("WdN", 0, 144), v("Wd", 0, 144), AF.Identity, scale=-65536.0)
    cols([6, 7, 8, 12])
    act(v("idf", 0, 112), v("ramp", 0, 112), AF.Identity, bias=col(16))
    cp(v("idb", 0, 112), v("idf", 0, 112), "s")
    guests("W0")
    for h in range(2):
        ts(v("CP", 128 * h, 128 * h + 128), v("val", 0, 128), col(10 + h), col(12), A.is_equal, A.mult)
    cp(v("Le", 0, w0), v("Se", 0, w0))
    cp(v("Lo", 0, w0), v("So", 0, w0))

    def cand_sums():
        for b in range(2):
            mm([(psv(6 + b, 0, 512), v("CP", 128 * h, 128 * h + 128), v("X", 1024 * h + 512 * b, 1024 * h + 512 * b + 512),
                 h == 0, h == 1) for h in range(2)])

    def cand_list(t, lo, hi):
        tt(v("cK", lo, hi), psv(6, lo, hi), v("nK%d" % t, lo, hi), A.min if t else A.max)
        ts(v("Lc", lo, hi), v("cK", lo, hi), -KEY, None, A.add)

    gather("s", v("X", 0, P), v("TG0", 0, 256), v("gam", 0, 128))
    cand_sums()
    ts(v("I1", 0, 128), v("val", 0, 128), 0.0, None, A.is_equal)
    cols([4, 5, 9, 10, 11, 13])
    ts(v("I16", 0, 128), v("val", 0, 128), 0.0, None, A.is_equal)
    ts(v("BO", 0, 128), v("qg", 0, 128), GI, -256.0, A.is_equal, A.mult)
    ts(v("nK0", 0, 256), v("ramp", 0, 256), col(15), None, A.add)
    tt(v("idb", 128, 240), v("idf", 0, 112), v("idb", 0, 112), A.subtract)
    for h in range(2):
        ts(v("BH", 128 * h, 128 * h + 128), v("val2", 0, 128), col(13 + h), 2 * KEY, A.is_equal, A.mult)
    tt(v("Wd2", 1, 144), v("Wd", 1, 144), v("Wd", 0, 143), A.add)
    for h in range(2):
        ts(v("nu", 64 * h, 64 * h + 64), v("ramp", 0, 64), col(17), 1024.0 * h, A.add, A.add)

    def own_names(t, lo):
        iota(v("Y", 0, P), [[1, P]], int(KEY) + W * t, 0)
        dmas([(v("nK%d" % t, lo, 1024, part=slice(h, 128, 2)), v("Y", 1024 * h + lo, 1024 * h + 1024, part=slice(h, 128, 2)))
              for h in range(2)])

    iota(v("one", 0, 512), [[0, 512]], 1, 0)
    iota(v("neg", 0, 128), [[0, 128]], -8, 0)
    own_names(0, 256)
    iota(v("cz", 0, 128), [[0, 128]], 7936, 0)
    iota(v("DA", 0, 1920), [[0, 1920]], 0, 0)
    for name, c in (("Ip", -16), ("In", 16)):
        iota(v(name, 0, 128), [[0, 128]], c, 0)
        order("g", [v(name, 0, 128)], [v(name, 0, 128)], nxt("g"))
        done("g", g.affine_select(T[name][:, 0:128], T[name][:, 0:128], [[-1, 128]], A.is_equal, 0.0, 0, 1))

    def pi_lists(t, items):
        dmas([(v("LP%d" % t, 128 * j + 64 * h, 128 * j + 64 * h + 64), v(src, 0, 1024, part=slice(2 * k + h, 128, 16)))
              for j, src, k in items for h in range(2)])

    def select_sum(lo, hi, bank):
        items = []
        for m0, w in zip(starts, CH):
            if lo <= m0 < hi:
                for h in range(2):
                    items.append((psv(bank, m0 - lo, m0 - lo + w), v("BH", 128 * h, 128 * h + 128),
                                  v("lt", 2 * m0 + h * w, 2 * m0 + (h + 1) * w), h == 0, h == 1))
        mm(items)

    def select(t, lo, hi, bank):
        tt(psv(bank, 0, hi - lo), v("cK", lo, hi), psv(bank, 0, hi - lo), A.subtract)
        tt(v("selI", lo, hi), psv(bank, 0, hi - lo), v("Se" if t else "So", lo, hi), A.max)
        ts(v("selI", lo, hi), v("selI", lo, hi), int(KEY) - 1, None, A.bitwise_and)
        cp(v("Ln%d" % t, lo, hi), v("selI", lo, hi))

    def extract(out, src, lo, n):
        mm([(out, to_a(a), v(src, lo + a, lo + 16 * n, 16), a == 0, a == 15) for a in range(16)])

    def mb(o):
        return (T.Mb[:, o, :], "Mb", 128 * o, 128 * o + 128)

    def keys_of(t):
        LP = "LP%d" % t
        if t == 0:
            ts(v("KP", 0, 128), v(LP, 0, 128), 3 * KEY, None, A.add)
            ts(v("KP", 128, 256), v(LP, 128, 256), KEY, None, A.add)
            cp(v("KP", 256, 384), v(LP, 256, 384))
            ts(v("KP", 384, 512), v(LP, 384, 512), KEY, None, A.add)
        else:
            ts(v("sf", 0, 128), v(LP, 384, 512), float(W), -float(W), A.is_ge, A.mult)
            ts(v("sf", 128, 256), v(LP, 384, 512), KEY, None, A.add)
            ts(v("sf", 256, 384), v("NL", 384, 512), float(P), -float(W), A.is_ge, A.mult)
            ts(v("sf", 384, 512), v("NL", 384, 512), float(W - P), None, A.add)
            tt(v("KP", 384, 512), v("sf", 0, 128), v("sf", 128, 256), A.add)
            tt(v("sf", 256, 384), v("sf", 256, 384), v("sf", 384, 512), A.add)
            cp(v("ZL", 0, 128), v("sf", 256, 384))

    def true_arcs(j, bank):
        if j < 2:
            cp(v("LU", 128 * j, 128 * j + 128), psv(bank, 0, 128))
        ts(v("KP", 128 * j, 128 * j + 128), psv(bank, 0, 128), [3 * KEY, KEY, 0.0][j], None, A.add)

    for t in range(2):
        win = v("T1", 0, W + P) if t else v("W0", 0, W)
        LK, LC = ("Ln0", "Le") if t else ("Le", "Lo")
        nq = len(CH)

        def worth(q):
            m0, w = starts[q], CH[q]
            b = q % 2
            ts(v("aI", 512 * b, 512 * b + 2 * w), psv(b, 0, 2 * w), -HALF, 255.0, A.add, A.min)
            ts(v("b16", 512 * b, 512 * b + 2 * w), psv(2 + b, 0, 2 * w), 1024.0 - HALF, 1279.0, A.add, A.min)
            tt(v("lt", 2 * m0, 2 * m0 + 2 * w), psv(2 + b, 0, 2 * w), v("aI", 512 * b, 512 * b + 2 * w), A.is_lt)

        def better(q):
            m0, w = starts[q], CH[q]
            b = q % 2
            mm([(psv(4 + b, 0, 2 * w), v("neg", 0, 128), v("one", 0, 2 * w), True, False),
                (psv(4 + b, 0, 2 * w), v("I16", 0, 128), v("b16", 512 * b, 512 * b + 2 * w), False, False),
                (psv(4 + b, 0, 2 * w), v("BO", 0, 128), v("lt", 2 * m0, 2 * m0 + 2 * w), False, True)])

        def newv(q):
            m0, w = starts[q], CH[q]
            b = q % 2
            for h in range(2):
                tt(v("U", 1024 * h + m0, 1024 * h + m0 + w), psv(4 + b, h * w, h * w + w),
                   v("aI", 512 * b + h * w, 512 * b + h * w + w), A.max)
            if t == 0 and q == 0:
                ghosts_out(1, "T1", v("U", 0, GH))
                ghosts_on(1, "T1")
                own_names(1, 0)

        def sums(bank, buf, par, w, first, last, rq):
            items = []
            if first:
                items.append((psv(bank, 0, 2 * w), v("I1", 0, 128), rq, True, False))
            for k in range(8):
                for h in range(2):
                    items.append((psv(bank, h * w, h * w + w), mb(2 * k + par), v(buf, 2 * k + h, 16 * w, 16),
                                  False, last and k == 7 and h == 1))
            mm(items)

        for q in range(nq):
            m0, w = starts[q], CH[q]
            b = q % 2
            gk, gc_, gb = "G%d" % b, "G%d" % (2 + b), "G%d" % (4 + b)
            rq = v("Rq", 2 * m0, 2 * m0 + 2 * w)
            sc, sb = PRM["SC"][t][q], PRM["SB"][t][q]
            gather("s", v(gk, 0, 16 * w), win, v(LK, m0, m0 + w))
            gather("s", v(gc_, 0, 16 * sc), win, v(LC, m0, m0 + sc))
            gather("v", v(gc_, 16 * sc, 16 * w), win, v(LC, m0 + sc, m0 + w))
            if q == 0:
                if t == 1:
                    gather("s", v("X", 0, P), v("TG1", 0, 256), v("gam", 0, 128))
                    gather("v", v("G6", 0, P), v("DB", 0, W), v("LP1", 0, 128))
                    gather("s", v("G7", 0, P), v("DB", 0, W), v("LP1", 128, 256))
                    cand_sums()
                cand_list(t, 0, 256)
                if t == 0:
                    cp(v("Le", w0, 1024), v("Se", w0, 1024))
            sums(b, gk, t, w, True, False, rq)
            sums(2 + b, gk, t, w, True, False, rq)
            if q >= 2:
                newv(q - 2)
            if q >= 1:
                worth(q - 1)
                better(q - 1)
            if q == 2 and PRM["SEL"]:
                select_sum(0, PRM["SEL"], 6)
            sums(b, gc_, 1 - t, w, False, True, rq)
            gather("s", v(gb, 0, 16 * sb), win, v("Lc", m0, m0 + sb))
            gather("v", v(gb, 16 * sb, 16 * w), win, v("Lc", m0 + sb, m0 + w))
            sums(2 + b, gb, 1 - t, w, False, True, rq)
            if q == 0:
                if t == 0:
                    cp(v("Lo", w0, 1024), v("So", w0, 1024))
                cand_list(t, 256, 1024)
                if t == 0:
                    cp(v("Lg", 0, 128), v("LgI", 0, 128))
                    pi_lists(0, [(0, "Le", 0), (1, "Le", 3), (2, "Lo", 1), (3, "Lc", 1)])
                    dmas([(v("DA", 1920, W), v("DA", 0, 1920))])
                    dmas([(v("U", P, W), v("W0", P, W))])
                    dmas([(v("DA", P, W, part=slice(c, 128, 16)), v("idb", 128 * c, 128 * c + 112)) for c in range(2)])
                    dmas([(v("DB", P, W), v("DA", P, W)), (v("F", P, W), v("DA", P, W))])
                else:
                    pi_lists(1, [(3, "Lc", 2)])
                    extract(psv(6, 0, 128), "G6", 0, 128)
                    extract(psv(7, 0, 128), "G7", 0, 128)
            if q == 1:
                keys_of(t)
                if t == 1:
                    true_arcs(0, 6)
                    true_arcs(1, 7)
            if q == 2:
                if PRM["SEL"]:
                    select(t, 0, PRM["SEL"], 6)
                if t == 1:
                    gather("s", v("G6", 0, P), v("DB", 0, W), v("LP1", 256, 384))
                    extract(psv(7, 0, 128), "G6", 0, 128)
            if q == 3 and t == 1:
                true_arcs(2, 7)
        newv(nq - 2)
        worth(nq - 1)
        better(nq - 1)
        newv(nq - 1)
        if t == 0:
            dmas([(v("T1", W, W + P), v("U", 0, P))])
        else:
            out_tok = dmas([(T.yv[:, :], v("U", 0, P))])

        for h in range(2):
            items = []
            for m0, w in zip(starts, CH):
                for c0 in range(m0, m0 + w, 64):
                    lo = 2 * m0 + h * w + c0 - m0
                    items.append((psv(7, 64 * h, 64 * h + 64), to_a(c0 // 64, "WdS"), v("lt", lo, lo + 64), c0 == 0, c0 == 960))
            mm(items)
        uwin = v("U", 0, W)
        pieces = [(j, m0) for j in range(3) for m0 in (0, 64)]

        def own_side(i):
            for hb in range(2):
                n0 = 16 * pieces[i][1] + 512 * hb
                mm([(psv(2 * (i % 3) + hb, 0, 512), v("In", 0, 128), v("U", n0, n0 + 512), True, False)])

        def diff(i):
            for hb in range(2):
                mm([(v("ps", 1024 * (i % 3) + 64 * a, 1024 * (i % 3) + 64 * a + 64), v("Ip", 0, 128), v("G%d" % i, a, 1024, 16),
                     False, a % 8 == 7) for a in range(8 * hb, 8 * hb + 8)])

        def ramp_up(q_, i, hb):
            o = v("cl", 1024 * (i % 3) + 512 * hb, 1024 * (i % 3) + 512 * hb + 512)
            src = psv(2 * (i % 3) + hb, 0, 512)
            if q_ == "v":
                ts(o, src, 1.0, 0.0, A.add, A.max)
            else:
                act(o, src, AF.Relu, bias=1.0)

        def zsum(i):
            j, m0 = pieces[i]
            c0 = 1024 * (i % 3)
            o = psv(6, 128 * j + m0, 128 * j + m0 + 64) if j < 2 else psv(7, 128 + m0, 128 + m0 + 64)
            mm([(o, v("cz", 0, 128), v("one", 0, 64), True, False)]
               + [(o, to_a(a, "WdN"), v("cl", c0 + 64 * a, c0 + 64 * a + 64), False, a == 15) for a in range(16)])

        for wd in PRM["DOM"].split():
            if wd[0] in "gh":
                i = int(wd[2])
                j, m0 = pieces[i]
                c0, c1 = (0, 64) if wd[0] == "g" else (32 * int(wd[3]), 32 * int(wd[3]) + 32)
                gather(wd[1], v("G%d" % i, 16 * c0, 16 * c1), uwin,
                       v("LP0" if (t == 0 and j < 2) else "LU", 128 * j + m0 + c0, 128 * j + m0 + c1))
            elif wd[0] == "p":
                own_side(int(wd[1]))
            elif wd[0] == "d":
                diff(int(wd[1]))
            elif wd[0] == "r":
                ramp_up(wd[1], int(wd[2]), int(wd[3]))
            elif wd[0] == "z":
                zsum(int(wd[1]))
            elif wd == "L":
                tt(psv(7, 0, 128), v("KP", 384, 512), psv(7, 0, 128), A.subtract)
                tt(v("si", 0, 128), psv(7, 0, 128), v("KP", 256, 384), A.max)
                ts(v("si", 0, 128), v("si", 0, 128), int(KEY) - 1, None, A.bitwise_and)
                cp(v("LU", 256, 384), v("si", 0, 128))
            elif wd == "K":
                ts(v("KP", 512, 640), v("si", 0, 128), 2 * KEY, None, A.add)
            elif wd == "P":
                tt(psv(6, 0, 256), psv(6, 0, 256), v("KP", 0, 256), A.min)
                tt(v("sf", 128, 256), psv(6, 0, 128), v("nu", 0, 128), A.max)
                tt(v("sf", 256, 384), psv(6, 128, 256), v("sf", 128, 256), A.max)
        if t == 0:
            dmas([(v("U", P, W), v("T1", P, W))])
        tt(psv(7, 128, 256), psv(7, 128, 256), v("KP", 512, 640), A.min)
        tt(v("si", 128, 256), psv(7, 128, 256), v("sf", 256, 384), A.max)
        ts(v("si", 128, 256), v("si", 128, 256), int(KEY) - 1, None, A.bitwise_and)
        cp(v("HL", 0, 128), v("si", 128, 256))
        tt(v("HL", 128, 256), v("si", 128, 256), v("HL", 0, 128), A.subtract)
        dmas([(v("DA", 1024 * h, 1024 * h + 1024, part=slice(c, 128, 16)), v("HL", 128 * c + 64 * h, 128 * c + 64 * h + 64))
              for c in range(2) for h in range(2)])
        lo = PRM["SEL"]
        while lo < 1024:
            hi = 512 if lo < 512 else 1024
            select_sum(lo, hi, lo // 512)
            select(t, lo, hi, lo // 512)
            lo = hi
        if t == 0:
            pi_lists(1, [(0, "Ln0", 0), (1, "Ln0", 3), (2, "Le", 2)])

        steps = [("DA", 0, "DB", 0), ("DB", 0, "DA", 0), ("DA", 0, "F" if t else "DB", W if t else 0)]
        if t == 0:
            steps.append(("DB", 1, "T1", 0))
        cv = PRM["CV"]
        for s, (src, last, dst, off) in enumerate(steps):
            l0 = 512 * t + 128 * s
            w_ = uwin if last else v(src, 0, W)
            for hf in range(2):
                extract(psv(6 + hf, 0, 64), src, 1024 * hf, 64)
            if last:
                gather("s", v("G6", 896, P), v("DB", 0, W), v("Lg", 56, 128))
                gather("v", v("G6", 0, 896), v("DB", 0, W), v("Lg", 0, 56))
            for hf in range(2):
                cp(v("NL", l0 + 64 * hf, l0 + 64 * hf + 64), psv(6 + hf, 0, 64))
                for q_, c0, c1 in (("v", 64 * hf, 64 * hf + cv), ("s", 64 * hf + cv, 64 * hf + 64)):
                    gather(q_, v(dst, off + 16 * c0, off + 16 * c1), w_, v("NL", l0 + c0, l0 + c1))
            if last:
                for h2 in range(2):
                    mm([(psv(5, 128 * h2, 128 * h2 + 128), to_a(2 * k, "Wd2"), v("G6", 2 * k + h2, P, 16), k == 0, k == 7)
                        for k in range(8)])
                make_table(1, psv(5, 0, 256))
                guests("U")

    for e, q_ in enumerate("vs"):
        gather(q_, v("F", 1024 * e, 1024 * e + 1024), v("F", P, W + P), v("ZL", 64 * e, 64 * e + 64))
    fwin = v("F", 0, W + P)
    FIN = PRM["FIN"]
    fs = [sum(FIN[:i]) for i in range(len(FIN) + 1)]

    def out_pair(i):
        for k in (i, i + 1):
            cp(v("Y", fs[k], fs[k + 1]), psv(k % 8, 0, FIN[k]), "vs"[k % 2])
        par, m0, n = (1 if fs[i] < 1024 else 0), fs[i] % 1024, fs[i + 2] - fs[i]
        dmas([(T.ys[par:128:2, 1024 * h + m0:1024 * h + m0 + n], v("Y", fs[i], fs[i + 2], part=slice(h, 128, 2)))
              for h in range(2)], tok=out_tok)

    for i, n in enumerate(FIN):
        name, m0 = ("Ln0" if fs[i] < 1024 else "Ln1"), fs[i] % 1024
        buf = "G%d" % (i % 6)
        gather("vs"[i % 2], v(buf, 0, 16 * n), fwin, v(name, m0, m0 + n))
        extract(psv(i % 8, 0, n), buf, 0, n)
        if i >= 3 and i % 2 == 1:
            out_pair(i - 3)
    out_pair(len(FIN) - 2)

    for name in total:
        if name != out_tok[0] and max(waited[q].get(name, 0) for q in Q) < total[name]:
            wait("g", [name, total[name]])
    wait("y", out_tok)
